import numpy as np, ml_dtypes
CORES = [44,45,46,47,172,173,174,175,300,301,302,303,428,429,430,431]
N = 16
import mx_ref
NC, G, MB, ROOT = 128, 2, 2, 11
C = np.float32(0.029)
BF = ml_dtypes.bfloat16
def cut(t, i, w=512):
    return t[:, w * i:w * i + w]
def tile(rs):
    return np.stack(rs, axis=2).reshape(128, -1).astype(BF)
def layer(w, X):
    out = []
    for i in range(G):
        for t in range(len(X)):
            p = mx_ref.matmul(mx_ref.quantize(cut(w, len(X) * i + t)), X[t])
            z = p if t == 0 else z + p
        out.append(z)
    return out
def act(Z):
    return [np.maximum(s * z, 0) * C for z in Z for s in (1, -1)]
def setup_inputs(rng):
    def f(*shape):
        return mx_ref.flush((rng.standard_normal(shape, dtype=np.float32) * np.exp2(rng.integers(-2, 3, shape[:-1] + (1,)))).astype(BF))
    return {"x": f(N, 128, MB * 4 * NC), "w1": f(N, 128, G * 512), "w2": f(N, 128, 512)}
def setup_inputs_blocks(rng):
    d = setup_inputs(rng)
    for k in ("x", "w1", "w2"): d[k] = mx_ref.spread(d[k], rng, 4)
    return d
def setup_inputs_wide(rng):
    d = setup_inputs(rng)
    for k in ("x", "w1", "w2"): d[k] = mx_ref.flush((d[k].astype(np.float32) * np.exp2(rng.integers(-8, 9, (N, 1, 1))).astype(np.float32)).astype(BF))
    return d
def setup_inputs_zeros(rng):
    d = setup_inputs(rng); v = d["x"].reshape(N, 128, -1, 4).copy()
    v[np.broadcast_to((rng.random((N, 1, v.shape[2], 1)) < 0.33), v.shape)] = 0
    d["x"] = v.reshape(d["x"].shape)
    return d
def reference(x, w1, w2):
    H = [mx_ref.quantize(tile(act(layer(w1[ROOT], [mx_ref.quantize(cut(x[ROOT], m, 4 * NC))])))) for m in range(MB)]
    y = np.zeros((N, 128, MB * NC), np.float32)
    for r in range(N):
        qw = mx_ref.quantize(w2[r])
        for m in range(MB):
            y[r][:, NC * m:NC * m + NC] = mx_ref.matmul(qw, H[m])
    return {"y": y}

@@ -1,0 +1,205 @@
+from concourse.bass import DstId, RemoteDMATransfer
+from concourse.mybir import dt, AluOpType, ActivationFunctionType
+
+C = 0.029
+NC = 128
+PIECES = 4
+WORDS = 86
+WIDTH = 4 * WORDS
+WORLD = 512
+CODES, PLANE = "float8_e4m3fn_x4", "uint8"
+
+SCRATCH = {
+    "xs": ("sbuf", [128, 1024], "bfloat16"),
+    "w1s": ("sbuf", [128, 1024], "bfloat16"),
+    "w2s": ("sbuf", [128, 512], "bfloat16"),
+    "h": ("sbuf", [128, 1024], "bfloat16"),
+    "rq": ("sbuf", [128, 512], CODES),
+    "rp": ("sbuf", [128, 512], PLANE),
+    "w1q": ("sbuf", [128, 256], CODES),
+    "w1p": ("sbuf", [128, 256], PLANE),
+    "w2q": ("sbuf", [128, 128], CODES),
+    "w2p": ("sbuf", [128, 128], PLANE),
+    "hq": ("sbuf", [128, 3 * WORDS], CODES),
+    "hp": ("sbuf", [128, WIDTH], PLANE),
+    "ys": ("sbuf", [128, 256], "float32"),
+    "z": ("psum", [128, 2048], "float32"),
+    "yp": ("psum", [128, 1024], "float32"),
+}
+SEMAPHORES = ["lx", "lw1", "lw2", "qx0", "qx1", "qw10", "qw11", "qw2", "z00", "z01", "z10", "z11",
+              "s0", "s1", "v0", "v1", "qh0", "qh1", "inp", "arr", "sent", "y0", "y1", "c0", "c1", "st0", "st1"]
+
+
+def piece(T, codes, plane, u):
+    if u < 3:
+        return codes[:, u * WORDS:(u + 1) * WORDS].bitcast(dt.uint8)
+    return plane[:, 0:WIDTH]
+
+
+def bits(mask):
+    return [b for b in range(16) if mask >> b & 1]
+
+
+def chip_cores(c, topo):
+    return [d for d in range(WORLD) if topo.host(d) == topo.host(c) and topo.chip(d) == topo.chip(c)]
+
+
+def relays_of(T, topo, seat, root):
+    groups = {}
+    for c in chip_cores(seat, topo):
+        owner = any(topo.mates(c, d) and topo.may_write(c, d) for d in range(WORLD))
+        groups.setdefault((topo.die(c), owner), []).append(c)
+    out = []
+    for key in sorted(groups):
+        cand = [c for c in groups[key] if c != root]
+        ranks = [c for c in cand if T.rank_of(c) is not None]
+        out.append((ranks or cand)[0])
+    return out
+
+
+def plan(T, topo):
+    root = T.cores[T.root]
+    near = [c for c in T.cores if topo.host(c) == topo.host(root)]
+    next_ = [c for c in T.cores if topo.host(c) != topo.host(root) and topo.rack(topo.host(c)) == topo.rack(topo.host(root))]
+    out = []
+    for home in (near, next_):
+        far = [c for c in T.cores if topo.rack(topo.host(c)) != topo.rack(topo.host(home[0])) and topo.may_write(home[0], c)]
+        out.append((relays_of(T, topo, home[0], root), [c for c in home if c != root], far))
+    return out
+
+
+def dst(topo, d, src):
+    rid, pid = topo.addr(d, src)
+    return DstId(rid=rid, pnc=pid)
+
+
+def split_masks(src, on, off, topo):
+    away = topo.mask(src, off)
+    return topo.mask(src, on) & ~away, away
+
+
+def rank_program(g, core, T, topo):
+    rank = T.rank_of(core)
+    root = T.cores[T.root]
+    groups = plan(T, topo)
+    if rank is not None:
+        finish(g, core, T, topo, groups, root)
+    if core == root:
+        root_send(g, core, T, topo, groups)
+        return
+    for relays, ranks, far in groups:
+        if core in relays:
+            u = relays.index(core)
+            on = [d for d in ranks if d != core]
+            m_on, m_off = split_masks(core, on[0], far[0], topo)
+            g.wait_ge(T.sem.inp, 2)
+            tr = []
+            for dests, m in ((far, m_off), (on, m_on)):
+                tr.append(RemoteDMATransfer(
+                    dst_ids=[dst(topo, d, core) for d in dests], dma_engine_mask=m, remote_sem=T.sem.arr,
+                    srcs=[piece(T, T.hq, T.hp, u)], dsts=[piece(T, T.hq, T.hp, u) for d in dests]))
+            g.remote_dma_fused(tr, local_sem=T.sem.sent)
+            g.wait_ge(T.sem.sent, len(bits(m_on)) + len(bits(m_off)))
+
+
+def root_send(g, core, T, topo, groups):
+    near, next_ = groups[0][0], groups[1][0]
+    m_on, m_off = split_masks(core, near[0], next_[0], topo)
+    e_on, e_off = bits(m_on), bits(m_off)
+    order = sorted(range(PIECES), key=lambda u: topo.die(near[u]) == topo.die(core))
+    slots = [e_on[0:4:2], e_on[4:8:2], e_on[1:4:2], e_on[5:8:2]]
+    mine = {u: slots[k] for k, u in enumerate(order)}
+    tr = []
+    for relays, engines in ((next_, lambda u: e_off[2 * u:2 * u + 2]), (near, lambda u: mine[u])):
+        for u in range(PIECES):
+            tr.append(RemoteDMATransfer(
+                dst_ids=[dst(topo, relays[u], core)], dma_engine_mask=sum(1 << e for e in engines(u)), remote_sem=T.sem.inp,
+                srcs=[piece(T, T.rq, T.rp, u)], dsts=[piece(T, T.hq, T.hp, u)]))
+    g.wait_ge(T.sem.qx0, 1)
+    g.wait_ge(T.sem.qx1, 1)
+    g.wait_ge(T.sem.qh0, 1)
+    g.wait_ge(T.sem.qh1, 1)
+    g.remote_dma_fused(tr, local_sem=T.sem.sent)
+    g.wait_ge(T.sem.sent, 16)
+
+
+def make_h(g, T):
+    s = T.sem
+    g.sync.dma_start(T.xs[:], T.x[:]).then_inc(s.lx, 16)
+    g.scalar.dma_start(T.w1s[:], T.w1[:]).then_inc(s.lw1, 16)
+
+    def quantise(q, p, at, src, col, sem):
+        g.vector.quantize_mx(q[:, at:at + NC], p[:, at:at + NC], src[:, col:col + 4 * NC]).then_inc(sem, 1)
+    g.vector.wait_ge(s.lx, 16)
+    quantise(T.rq, T.rp, 256, T.xs, 0, s.qx0)
+    g.vector.wait_ge(s.lw1, 16)
+    quantise(T.w1q, T.w1p, 0, T.w1s, 0, s.qw10)
+    quantise(T.w1q, T.w1p, NC, T.w1s, 512, s.qw11)
+    quantise(T.rq, T.rp, 256 + NC, T.xs, 512, s.qx1)
+
+    def product(i, m, sem):
+        b = 512 * (2 * i + m)
+        w, c = slice(NC * i, NC * i + NC), slice(256 + NC * m, 256 + NC * m + NC)
+        g.tensor.matmul_mx(T.z[:, b:b + NC], T.w1q[:, w], T.w1p[:, w], T.rq[:, c], T.rp[:, c], True, True).then_inc(sem, 1)
+    g.tensor.wait_ge(s.qx0, 1)
+    g.tensor.wait_ge(s.qw10, 1)
+    product(0, 0, s.z00)
+    g.tensor.wait_ge(s.qw11, 1)
+    product(1, 0, s.z10)
+    g.tensor.wait_ge(s.qx1, 1)
+    product(0, 1, s.z01)
+    product(1, 1, s.z11)
+
+    for m, zs, zv, ss, sv, qh in ((0, s.z00, s.z10, s.s0, s.v0, s.qh0), (1, s.z01, s.z11, s.s1, s.v1, s.qh1)):
+        lo, hi = 512 * m, 512 * m + 512
+        z0, z1 = T.z[:, lo:lo + NC], T.z[:, 1024 + lo:1024 + lo + NC]
+        g.scalar.wait_ge(zs, 1)
+        g.scalar.activation(T.h[:, lo:hi:4], z0, ActivationFunctionType.Relu, scale=C).then_inc(ss, 1)
+        g.scalar.activation(T.h[:, lo + 1:hi:4], z0, ActivationFunctionType.Relu, scale=-C).then_inc(ss, 1)
+        g.vector.wait_ge(zv, 1)
+        g.vector.tensor_scalar(T.h[:, lo + 2:hi:4], z1, 0.0, C, AluOpType.max, AluOpType.mult).then_inc(sv, 1)
+        g.vector.tensor_scalar(T.h[:, lo + 3:hi:4], z1, -C, 0.0, AluOpType.mult, AluOpType.max).then_inc(sv, 1)
+        g.vector.wait_ge(ss, 2)
+        g.vector.wait_ge(sv, 2)
+        quantise(T.rq, T.rp, NC * m, T.h, lo, qh)
+
+
+def finish(g, core, T, topo, groups, root):
+    s = T.sem
+    if core == root:
+        make_h(g, T)
+        g.sync.wait_ge(s.lx, 16)
+        g.sync.wait_ge(s.lw1, 16)
+    g.sync.dma_start(T.w2s[:], T.w2[:]).then_inc(s.lw2, 16)
+    g.vector.wait_ge(s.lw2, 16)
+    g.vector.quantize_mx(T.w2q[:], T.w2p[:], T.w2s[:]).then_inc(s.qw2, 1)
+    g.tensor.wait_ge(s.qw2, 1)
+    if core == root:
+        q, p = T.rq, T.rp
+        g.tensor.wait_ge(s.qh0, 1)
+        g.tensor.wait_ge(s.qh1, 1)
+    else:
+        q, p = T.hq, T.hp
+        total = 0
+        for relays, ranks, far in groups:
+            if core in ranks or core in far:
+                for rl in relays:
+                    if rl == core:
+                        g.tensor.wait_ge(s.inp, 2)
+                    else:
+                        m_on, m_off = split_masks(rl, [d for d in ranks if d != rl][0], far[0], topo)
+                        total += len(bits(m_on if core in ranks else m_off))
+        g.tensor.wait_ge(s.arr, total)
+    for m, sem in ((0, s.y0), (1, s.y1)):
+        c = slice(NC * m, NC * m + NC)
+        g.tensor.matmul_mx(T.yp[:, 512 * m:512 * m + NC], T.w2q[:], T.w2p[:], q[:, c], p[:, c], True, True).then_inc(sem, 1)
+    g.vector.wait_ge(s.y0, 1)
+    g.vector.tensor_copy(T.ys[:, 0:NC], T.yp[:, 0:NC]).then_inc(s.c0, 1)
+    g.sync.wait_ge(s.c0, 1)
+    g.sync.dma_start(T.y[:, 0:NC], T.ys[:, 0:NC]).then_inc(s.st0, 16)
+    g.sync.wait_ge(s.st0, 16)
+    g.scalar.wait_ge(s.y1, 1)
+    g.scalar.activation(T.ys[:, NC:2 * NC], T.yp[:, 512:512 + NC], ActivationFunctionType.Copy).then_inc(s.c1, 1)
+    g.scalar.wait_ge(s.c1, 1)
+    g.scalar.dma_start(T.y[:, NC:2 * NC], T.ys[:, NC:2 * NC]).then_inc(s.st1, 16)
+    g.scalar.wait_ge(s.st1, 16)

@@ -3,9 +3,7 @@ from concourse.mybir import dt, AluOpType, ActivationFunctionType
 
 C = 0.029
 NC = 128
-PIECES = 4
-WORDS = 86
-WIDTH = 4 * WORDS
+CABLE, WORDS = 4, 48
 WORLD = 512
 CODES, PLANE = "float8_e4m3fn_x4", "uint8"
 
@@ -14,14 +12,14 @@ SCRATCH = {
     "w1s": ("sbuf", [128, 1024], "bfloat16"),
     "w2s": ("sbuf", [128, 512], "bfloat16"),
     "h": ("sbuf", [128, 1024], "bfloat16"),
-    "rq": ("sbuf", [128, 512], CODES),
-    "rp": ("sbuf", [128, 512], PLANE),
+    "xq": ("sbuf", [128, 256], CODES),
+    "xp": ("sbuf", [128, 256], PLANE),
     "w1q": ("sbuf", [128, 256], CODES),
     "w1p": ("sbuf", [128, 256], PLANE),
     "w2q": ("sbuf", [128, 128], CODES),
     "w2p": ("sbuf", [128, 128], PLANE),
-    "hq": ("sbuf", [128, 3 * WORDS], CODES),
-    "hp": ("sbuf", [128, WIDTH], PLANE),
+    "hq": ("sbuf", [128, 256], CODES),
+    "hp": ("sbuf", [128, 256], PLANE),
     "ys": ("sbuf", [128, 256], "float32"),
     "z": ("psum", [128, 2048], "float32"),
     "yp": ("psum", [128, 1024], "float32"),
@@ -30,41 +28,58 @@ SEMAPHORES = ["lx", "lw1", "lw2", "qx0", "qx1", "qw10", "qw11", "qw2", "z00", "z
               "s0", "s1", "v0", "v1", "qh0", "qh1", "inp", "arr", "sent", "y0", "y1", "c0", "c1", "st0", "st1"]
 
 
-def piece(T, codes, plane, u):
-    if u < 3:
-        return codes[:, u * WORDS:(u + 1) * WORDS].bitcast(dt.uint8)
-    return plane[:, 0:WIDTH]
+def piece(T, u):
+    if u < CABLE:
+        return T.hq[:, u * WORDS:(u + 1) * WORDS].bitcast(dt.uint8)
+    return T.hq[:, CABLE * WORDS:256].bitcast(dt.uint8) if u == CABLE else T.hp[:]
 
 
 def bits(mask):
     return [b for b in range(16) if mask >> b & 1]
 
 
-def chip_cores(c, topo):
-    return [d for d in range(WORLD) if topo.host(d) == topo.host(c) and topo.chip(d) == topo.chip(c)]
+def mask_of(engines):
+    return sum(1 << e for e in engines)
 
 
-def relays_of(T, topo, seat, root):
+def pairs_of(c, topo):
     groups = {}
-    for c in chip_cores(seat, topo):
-        owner = any(topo.mates(c, d) and topo.may_write(c, d) for d in range(WORLD))
-        groups.setdefault((topo.die(c), owner), []).append(c)
-    out = []
-    for key in sorted(groups):
-        cand = [c for c in groups[key] if c != root]
-        ranks = [c for c in cand if T.rank_of(c) is not None]
-        out.append((ranks or cand)[0])
-    return out
+    for d in range(WORLD):
+        if topo.host(d) == topo.host(c) and topo.chip(d) == topo.chip(c):
+            owner = any(topo.mates(d, m) and topo.may_write(d, m) for m in range(WORLD))
+            groups.setdefault((topo.die(d), owner), []).append(d)
+    return groups
+
+
+def ranks_first(cores, T):
+    return sorted(cores, key=lambda c: T.rank_of(c) is None)
 
 
 def plan(T, topo):
     root = T.cores[T.root]
-    near = [c for c in T.cores if topo.host(c) == topo.host(root)]
-    next_ = [c for c in T.cores if topo.host(c) != topo.host(root) and topo.rack(topo.host(c)) == topo.rack(topo.host(root))]
-    out = []
-    for home in (near, next_):
-        far = [c for c in T.cores if topo.rack(topo.host(c)) != topo.rack(topo.host(home[0])) and topo.may_write(home[0], c)]
-        out.append((relays_of(T, topo, home[0], root), [c for c in home if c != root], far))
+
+    def at(test):
+        return [c for c in T.cores if c != root and test(c)]
+
+    def same_rack(a, b):
+        return topo.rack(topo.host(a)) == topo.rack(topo.host(b))
+    home = at(lambda c: topo.host(c) == topo.host(root))
+    side = at(lambda c: topo.host(c) != topo.host(root) and same_rack(c, root))
+    across = at(lambda c: not same_rack(c, root) and topo.may_write(root, c))
+    diagonal = at(lambda c: not same_rack(c, root) and not topo.may_write(root, c))
+    out, used = [], {root}
+    for ranks, far in ((home, across), (side, diagonal)):
+        groups = pairs_of(ranks[0], topo)
+        for u, key in enumerate(sorted(groups)):
+            relay = ranks_first([c for c in groups[key] if c not in used], T)[0]
+            used.add(relay)
+            out.append((relay, u, [d for d in ranks if d != relay], far))
+    for ranks, far in ((home, side), (across, diagonal)):
+        groups = pairs_of(ranks[0], topo)
+        for u, die in ((CABLE, 0), (CABLE + 1, 1)):
+            relay = ranks_first([c for key in sorted(groups) if key[0] == die for c in groups[key] if c not in used], T)[0]
+            used.add(relay)
+            out.append((relay, u, [d for d in ranks if d != relay], far))
     return out
 
 
@@ -73,54 +88,52 @@ def dst(topo, d, src):
     return DstId(rid=rid, pnc=pid)
 
 
-def split_masks(src, on, off, topo):
+def split_engines(src, on, off, topo):
     away = topo.mask(src, off)
-    return topo.mask(src, on) & ~away, away
+    return bits(topo.mask(src, on) & ~away), bits(away)
+
+
+def transfer(T, topo, src, dests, u, engines, sem):
+    return RemoteDMATransfer(dst_ids=[dst(topo, d, src) for d in dests], dma_engine_mask=mask_of(engines), remote_sem=sem,
+                             srcs=[piece(T, u)], dsts=[piece(T, u) for d in dests])
 
 
 def rank_program(g, core, T, topo):
-    rank = T.rank_of(core)
     root = T.cores[T.root]
-    groups = plan(T, topo)
-    if rank is not None:
-        finish(g, core, T, topo, groups, root)
+    routes = plan(T, topo)
+    if T.rank_of(core) is not None:
+        finish(g, core, T, topo, routes, root)
     if core == root:
-        root_send(g, core, T, topo, groups)
-        return
-    for relays, ranks, far in groups:
-        if core in relays:
-            u = relays.index(core)
-            on = [d for d in ranks if d != core]
-            m_on, m_off = split_masks(core, on[0], far[0], topo)
-            g.wait_ge(T.sem.inp, 2)
-            tr = []
-            for dests, m in ((far, m_off), (on, m_on)):
-                tr.append(RemoteDMATransfer(
-                    dst_ids=[dst(topo, d, core) for d in dests], dma_engine_mask=m, remote_sem=T.sem.arr,
-                    srcs=[piece(T, T.hq, T.hp, u)], dsts=[piece(T, T.hq, T.hp, u) for d in dests]))
-            g.remote_dma_fused(tr, local_sem=T.sem.sent)
-            g.wait_ge(T.sem.sent, len(bits(m_on)) + len(bits(m_off)))
+        root_send(g, core, T, topo, routes)
+    for relay, u, on, off in routes:
+        if core == relay:
+            e_on, e_off = split_engines(core, on[0], off[0], topo)
+            g.wait_ge(T.sem.inp, arrival(u))
+            g.remote_dma_fused([transfer(T, topo, core, off, u, e_off, T.sem.arr),
+                                transfer(T, topo, core, on, u, e_on, T.sem.arr)], local_sem=T.sem.sent)
+            g.wait_ge(T.sem.sent, len(e_on) + len(e_off))
 
 
-def root_send(g, core, T, topo, groups):
-    near, next_ = groups[0][0], groups[1][0]
-    m_on, m_off = split_masks(core, near[0], next_[0], topo)
-    e_on, e_off = bits(m_on), bits(m_off)
-    order = sorted(range(PIECES), key=lambda u: topo.die(near[u]) == topo.die(core))
-    slots = [e_on[0:4:2], e_on[4:8:2], e_on[1:4:2], e_on[5:8:2]]
-    mine = {u: slots[k] for k, u in enumerate(order)}
-    tr = []
-    for relays, engines in ((next_, lambda u: e_off[2 * u:2 * u + 2]), (near, lambda u: mine[u])):
-        for u in range(PIECES):
-            tr.append(RemoteDMATransfer(
-                dst_ids=[dst(topo, relays[u], core)], dma_engine_mask=sum(1 << e for e in engines(u)), remote_sem=T.sem.inp,
-                srcs=[piece(T, T.rq, T.rp, u)], dsts=[piece(T, T.hq, T.hp, u)]))
-    g.wait_ge(T.sem.qx0, 1)
-    g.wait_ge(T.sem.qx1, 1)
+def arrival(u):
+    return 2 if u < CABLE else 4
+
+
+def root_send(g, core, T, topo, routes):
+    near = [r for r in routes if topo.host(r[0]) == topo.host(core)]
+    away = [r for r in routes if topo.host(r[0]) != topo.host(core)]
+    e_on, e_off = split_engines(core, near[0][0], away[0][0], topo)
+    turns = e_on[0::2] + e_on[1::2]
     g.wait_ge(T.sem.qh0, 1)
     g.wait_ge(T.sem.qh1, 1)
-    g.remote_dma_fused(tr, local_sem=T.sem.sent)
-    g.wait_ge(T.sem.sent, 16)
+    for kind in (range(CABLE), range(CABLE, CABLE + 2)):
+        n = arrival(kind[0])
+        tr = []
+        for part, engines in (([r for r in away if r[1] in kind], e_off),
+                              (sorted([r for r in near if r[1] in kind], key=lambda r: topo.die(r[0]) == topo.die(core)), turns)):
+            for k, r in enumerate(part):
+                tr.append(transfer(T, topo, core, [r[0]], r[1], engines[n * k:n * k + n], T.sem.inp))
+        g.remote_dma_fused(tr, local_sem=T.sem.sent)
+    g.wait_ge(T.sem.sent, 2 * (len(e_on) + len(e_off)))
 
 
 def make_h(g, T):
@@ -128,19 +141,20 @@ def make_h(g, T):
     g.sync.dma_start(T.xs[:], T.x[:]).then_inc(s.lx, 16)
     g.scalar.dma_start(T.w1s[:], T.w1[:]).then_inc(s.lw1, 16)
 
-    def quantise(q, p, at, src, col, sem):
-        g.vector.quantize_mx(q[:, at:at + NC], p[:, at:at + NC], src[:, col:col + 4 * NC]).then_inc(sem, 1)
+    def quantise(q, p, i, src, sem):
+        g.vector.quantize_mx(q[:, NC * i:NC * i + NC], p[:, NC * i:NC * i + NC],
+                             src[:, 4 * NC * i:4 * NC * i + 4 * NC]).then_inc(sem, 1)
     g.vector.wait_ge(s.lx, 16)
-    quantise(T.rq, T.rp, 256, T.xs, 0, s.qx0)
+    quantise(T.xq, T.xp, 0, T.xs, s.qx0)
     g.vector.wait_ge(s.lw1, 16)
-    quantise(T.w1q, T.w1p, 0, T.w1s, 0, s.qw10)
-    quantise(T.w1q, T.w1p, NC, T.w1s, 512, s.qw11)
-    quantise(T.rq, T.rp, 256 + NC, T.xs, 512, s.qx1)
+    quantise(T.w1q, T.w1p, 0, T.w1s, s.qw10)
+    quantise(T.w1q, T.w1p, 1, T.w1s, s.qw11)
+    quantise(T.xq, T.xp, 1, T.xs, s.qx1)
 
     def product(i, m, sem):
         b = 512 * (2 * i + m)
-        w, c = slice(NC * i, NC * i + NC), slice(256 + NC * m, 256 + NC * m + NC)
-        g.tensor.matmul_mx(T.z[:, b:b + NC], T.w1q[:, w], T.w1p[:, w], T.rq[:, c], T.rp[:, c], True, True).then_inc(sem, 1)
+        w, c = slice(NC * i, NC * i + NC), slice(NC * m, NC * m + NC)
+        g.tensor.matmul_mx(T.z[:, b:b + NC], T.w1q[:, w], T.w1p[:, w], T.xq[:, c], T.xp[:, c], True, True).then_inc(sem, 1)
     g.tensor.wait_ge(s.qx0, 1)
     g.tensor.wait_ge(s.qw10, 1)
     product(0, 0, s.z00)
@@ -161,10 +175,10 @@ def make_h(g, T):
         g.vector.tensor_scalar(T.h[:, lo + 3:hi:4], z1, -C, 0.0, AluOpType.mult, AluOpType.max).then_inc(sv, 1)
         g.vector.wait_ge(ss, 2)
         g.vector.wait_ge(sv, 2)
-        quantise(T.rq, T.rp, NC * m, T.h, lo, qh)
+        quantise(T.hq, T.hp, m, T.h, qh)
 
 
-def finish(g, core, T, topo, groups, root):
+def finish(g, core, T, topo, routes, root):
     s = T.sem
     if core == root:
         make_h(g, T)
@@ -175,24 +189,19 @@ def finish(g, core, T, topo, groups, root):
     g.vector.quantize_mx(T.w2q[:], T.w2p[:], T.w2s[:]).then_inc(s.qw2, 1)
     g.tensor.wait_ge(s.qw2, 1)
     if core == root:
-        q, p = T.rq, T.rp
         g.tensor.wait_ge(s.qh0, 1)
         g.tensor.wait_ge(s.qh1, 1)
     else:
-        q, p = T.hq, T.hp
         total = 0
-        for relays, ranks, far in groups:
-            if core in ranks or core in far:
-                for rl in relays:
-                    if rl == core:
-                        g.tensor.wait_ge(s.inp, 2)
-                    else:
-                        m_on, m_off = split_masks(rl, [d for d in ranks if d != rl][0], far[0], topo)
-                        total += len(bits(m_on if core in ranks else m_off))
+        for relay, u, on, off in routes:
+            e_on, e_off = split_engines(relay, on[0], off[0], topo)
+            if core == relay:
+                g.tensor.wait_ge(s.inp, arrival(u))
+            total += (len(e_on) if core in on else 0) + (len(e_off) if core in off else 0)
         g.tensor.wait_ge(s.arr, total)
     for m, sem in ((0, s.y0), (1, s.y1)):
         c = slice(NC * m, NC * m + NC)
-        g.tensor.matmul_mx(T.yp[:, 512 * m:512 * m + NC], T.w2q[:], T.w2p[:], q[:, c], p[:, c], True, True).then_inc(sem, 1)
+        g.tensor.matmul_mx(T.yp[:, 512 * m:512 * m + NC], T.w2q[:], T.w2p[:], T.hq[:, c], T.hp[:, c], True, True).then_inc(sem, 1)
     g.vector.wait_ge(s.y0, 1)
     g.vector.tensor_copy(T.ys[:, 0:NC], T.yp[:, 0:NC]).then_inc(s.c0, 1)
     g.sync.wait_ge(s.c0, 1)

@@ -3,7 +3,8 @@ from concourse.mybir import dt, AluOpType, ActivationFunctionType
 
 C = 0.029
 NC = 128
-CABLE, WORDS = 4, 48
+CABLE = 4
+WORDS = NC // CABLE
 WORLD = 512
 CODES, PLANE = "float8_e4m3fn_x4", "uint8"
 
@@ -24,14 +25,17 @@ SCRATCH = {
     "z": ("psum", [128, 2048], "float32"),
     "yp": ("psum", [128, 1024], "float32"),
 }
-SEMAPHORES = ["lx", "lw1", "lw2", "qx0", "qx1", "qw10", "qw11", "qw2", "z00", "z01", "z10", "z11",
-              "s0", "s1", "v0", "v1", "qh0", "qh1", "inp", "arr", "sent", "y0", "y1", "c0", "c1", "st0", "st1"]
+SEMAPHORES = ["lx", "lw1", "lw2", "qx0", "qx1", "qw10", "qw11", "qw2", "z00", "z01", "z10", "z11", "s0", "s1", "v0", "v1", "qh0", "qh1",
+              "early", "inp", "arr0", "arr1", "sent", "y0", "y1", "c0", "c1", "st0", "st1"]
 
 
-def piece(T, u):
-    if u < CABLE:
-        return T.hq[:, u * WORDS:(u + 1) * WORDS].bitcast(dt.uint8)
-    return T.hq[:, CABLE * WORDS:256].bitcast(dt.uint8) if u == CABLE else T.hp[:]
+def codes(T, m, u):
+    a = NC * m + WORDS * u
+    return T.hq[:, a:a + WORDS].bitcast(dt.uint8)
+
+
+def plane(T, m):
+    return T.hp[:, NC * m:NC * m + NC]
 
 
 def bits(mask):
@@ -51,10 +55,6 @@ def pairs_of(c, topo):
     return groups
 
 
-def ranks_first(cores, T):
-    return sorted(cores, key=lambda c: T.rank_of(c) is None)
-
-
 def plan(T, topo):
     root = T.cores[T.root]
 
@@ -67,20 +67,32 @@ def plan(T, topo):
     side = at(lambda c: topo.host(c) != topo.host(root) and same_rack(c, root))
     across = at(lambda c: not same_rack(c, root) and topo.may_write(root, c))
     diagonal = at(lambda c: not same_rack(c, root) and not topo.may_write(root, c))
-    out, used = [], {root}
+    used = {root}
+
+    def take(groups, keys):
+        free = [c for key in keys for c in groups[key] if c not in used]
+        relay = sorted(free, key=lambda c: T.rank_of(c) is None)[0]
+        used.add(relay)
+        return relay
+
+    def others(ranks, c):
+        return [d for d in ranks if d != c]
+    firsts = []
     for ranks, far in ((home, across), (side, diagonal)):
         groups = pairs_of(ranks[0], topo)
-        for u, key in enumerate(sorted(groups)):
-            relay = ranks_first([c for c in groups[key] if c not in used], T)[0]
-            used.add(relay)
-            out.append((relay, u, [d for d in ranks if d != relay], far))
+        firsts += [(take(groups, [key]), u, ranks, far) for u, key in enumerate(sorted(groups))]
+    switch = []
     for ranks, far in ((home, side), (across, diagonal)):
         groups = pairs_of(ranks[0], topo)
-        for u, die in ((CABLE, 0), (CABLE + 1, 1)):
-            relay = ranks_first([c for key in sorted(groups) if key[0] == die for c in groups[key] if c not in used], T)[0]
-            used.add(relay)
-            out.append((relay, u, [d for d in ranks if d != relay], far))
-    return out
+        for m in (0, 1):
+            relay = take(groups, [key for key in sorted(groups) if key[0] == m])
+            switch.append((relay, m, others(ranks, relay), far))
+    cable = []
+    for relay, u, ranks, far in firsts:
+        groups = pairs_of(far[0], topo)
+        hand = take(groups, sorted(groups))
+        cable.append((relay, u, others(ranks, relay), far, hand, others(far, hand)))
+    return cable, switch
 
 
 def dst(topo, d, src):
@@ -93,47 +105,65 @@ def split_engines(src, on, off, topo):
     return bits(topo.mask(src, on) & ~away), bits(away)
 
 
-def transfer(T, topo, src, dests, u, engines, sem):
+def transfer(topo, src, dests, view, engines, sem):
     return RemoteDMATransfer(dst_ids=[dst(topo, d, src) for d in dests], dma_engine_mask=mask_of(engines), remote_sem=sem,
-                             srcs=[piece(T, u)], dsts=[piece(T, u) for d in dests])
+                             srcs=[view], dsts=[view for d in dests])
+
+
+N_CODES, N_PLANE = 2, 4
 
 
 def rank_program(g, core, T, topo):
     root = T.cores[T.root]
-    routes = plan(T, topo)
+    cable, switch = plan(T, topo)
+    s = T.sem
     if T.rank_of(core) is not None:
-        finish(g, core, T, topo, routes, root)
+        finish(g, core, T, topo, cable, switch, root)
     if core == root:
-        root_send(g, core, T, topo, routes)
-    for relay, u, on, off in routes:
+        root_send(g, core, T, topo, cable, switch)
+    for relay, u, on, off, hand, served in cable:
         if core == relay:
             e_on, e_off = split_engines(core, on[0], off[0], topo)
-            g.wait_ge(T.sem.inp, arrival(u))
-            g.remote_dma_fused([transfer(T, topo, core, off, u, e_off, T.sem.arr),
-                                transfer(T, topo, core, on, u, e_on, T.sem.arr)], local_sem=T.sem.sent)
-            g.wait_ge(T.sem.sent, len(e_on) + len(e_off))
+            g.wait_ge(s.early, N_CODES)
+            g.remote_dma_fused([transfer(topo, core, [hand], codes(T, 0, u), e_off, s.early)], local_sem=s.sent)
+            g.wait_ge(s.inp, N_CODES)
+            g.remote_dma_fused([transfer(topo, core, off, codes(T, 1, u), e_off, s.arr1),
+                                transfer(topo, core, on, codes(T, 1, u), e_on, s.arr1)], local_sem=s.sent)
+            g.remote_dma_fused([transfer(topo, core, on, codes(T, 0, u), e_on, s.arr0)], local_sem=s.sent)
+            g.wait_ge(s.sent, 2 * (len(e_on) + len(e_off)))
+        if core == hand:
+            engines = bits(topo.mask(core, served[0]))
+            g.wait_ge(s.early, len(split_engines(relay, on[0], off[0], topo)[1]))
+            g.remote_dma_fused([transfer(topo, core, served, codes(T, 0, u), engines, s.arr0)], local_sem=s.sent)
+            g.wait_ge(s.sent, len(engines))
+    for relay, m, on, off in switch:
+        if core == relay:
+            e_on, e_off = split_engines(core, on[0], off[0], topo)
+            sem = (s.arr0, s.arr1)[m]
+            g.wait_ge(s.inp, N_PLANE)
+            g.remote_dma_fused([transfer(topo, core, off, plane(T, m), e_off, sem),
+                                transfer(topo, core, on, plane(T, m), e_on, sem)], local_sem=s.sent)
+            g.wait_ge(s.sent, len(e_on) + len(e_off))
 
 
-def arrival(u):
-    return 2 if u < CABLE else 4
+def root_send(g, core, T, topo, cable, switch):
+    s = T.sem
 
-
-def root_send(g, core, T, topo, routes):
-    near = [r for r in routes if topo.host(r[0]) == topo.host(core)]
-    away = [r for r in routes if topo.host(r[0]) != topo.host(core)]
-    e_on, e_off = split_engines(core, near[0][0], away[0][0], topo)
+    def by_host(routes):
+        near = [r for r in routes if topo.host(r[0]) == topo.host(core)]
+        return (sorted(near, key=lambda r: topo.die(r[0]) == topo.die(core)),
+                [r for r in routes if topo.host(r[0]) != topo.host(core)])
+    e_on, e_off = split_engines(core, cable[0][0], by_host(cable)[1][0][0], topo)
     turns = e_on[0::2] + e_on[1::2]
-    g.wait_ge(T.sem.qh0, 1)
-    g.wait_ge(T.sem.qh1, 1)
-    for kind in (range(CABLE), range(CABLE, CABLE + 2)):
-        n = arrival(kind[0])
-        tr = []
-        for part, engines in (([r for r in away if r[1] in kind], e_off),
-                              (sorted([r for r in near if r[1] in kind], key=lambda r: topo.die(r[0]) == topo.die(core)), turns)):
-            for k, r in enumerate(part):
-                tr.append(transfer(T, topo, core, [r[0]], r[1], engines[n * k:n * k + n], T.sem.inp))
-        g.remote_dma_fused(tr, local_sem=T.sem.sent)
-    g.wait_ge(T.sem.sent, 2 * (len(e_on) + len(e_off)))
+    for ready, routes, n, view, sem in ((s.qh0, cable, N_CODES, lambda k: codes(T, 0, k), s.early),
+                                        (s.qh1, cable, N_CODES, lambda k: codes(T, 1, k), s.inp),
+                                        (None, switch, N_PLANE, lambda k: plane(T, k), s.inp)):
+        if ready is not None:
+            g.wait_ge(ready, 1)
+        near, away = by_host(routes)
+        g.remote_dma_fused([transfer(topo, core, [r[0]], view(r[1]), engines[n * k:n * k + n], sem)
+                            for part, engines in ((away, e_off), (near, turns)) for k, r in enumerate(part)], local_sem=s.sent)
+    g.wait_ge(s.sent, 3 * (len(e_on) + len(e_off)))
 
 
 def make_h(g, T):
@@ -164,21 +194,46 @@ def make_h(g, T):
     product(0, 1, s.z01)
     product(1, 1, s.z11)
 
-    for m, zs, zv, ss, sv, qh in ((0, s.z00, s.z10, s.s0, s.v0, s.qh0), (1, s.z01, s.z11, s.s1, s.v1, s.qh1)):
+    for m, zv, zs, ss, sv, qh in ((0, s.z00, s.z10, s.s0, s.v0, s.qh0), (1, s.z01, s.z11, s.s1, s.v1, s.qh1)):
         lo, hi = 512 * m, 512 * m + 512
         z0, z1 = T.z[:, lo:lo + NC], T.z[:, 1024 + lo:1024 + lo + NC]
-        g.scalar.wait_ge(zs, 1)
-        g.scalar.activation(T.h[:, lo:hi:4], z0, ActivationFunctionType.Relu, scale=C).then_inc(ss, 1)
-        g.scalar.activation(T.h[:, lo + 1:hi:4], z0, ActivationFunctionType.Relu, scale=-C).then_inc(ss, 1)
         g.vector.wait_ge(zv, 1)
-        g.vector.tensor_scalar(T.h[:, lo + 2:hi:4], z1, 0.0, C, AluOpType.max, AluOpType.mult).then_inc(sv, 1)
-        g.vector.tensor_scalar(T.h[:, lo + 3:hi:4], z1, -C, 0.0, AluOpType.mult, AluOpType.max).then_inc(sv, 1)
-        g.vector.wait_ge(ss, 2)
+        g.vector.tensor_scalar(T.h[:, lo:hi:4], z0, 0.0, C, AluOpType.max, AluOpType.mult).then_inc(sv, 1)
+        g.vector.tensor_scalar(T.h[:, lo + 1:hi:4], z0, -C, 0.0, AluOpType.mult, AluOpType.max).then_inc(sv, 1)
+        g.scalar.wait_ge(zs, 1)
+        g.scalar.activation(T.h[:, lo + 2:hi:4], z1, ActivationFunctionType.Relu, scale=C).then_inc(ss, 1)
+        g.scalar.activation(T.h[:, lo + 3:hi:4], z1, ActivationFunctionType.Relu, scale=-C).then_inc(ss, 1)
         g.vector.wait_ge(sv, 2)
+        g.vector.wait_ge(ss, 2)
         quantise(T.hq, T.hp, m, T.h, qh)
 
 
-def finish(g, core, T, topo, routes, root):
+def landing(core, T, topo, cable, switch):
+    s = T.sem
+    own, total = ([], []), [0, 0]
+    for relay, u, on, off, hand, served in cable:
+        e_on, e_off = split_engines(relay, on[0], off[0], topo)
+        if core == relay:
+            own[0].append((s.early, N_CODES))
+            own[1].append((s.inp, N_CODES))
+        if core == hand:
+            own[0].append((s.early, len(e_off)))
+        if core in on:
+            total[0] += len(e_on)
+            total[1] += len(e_on)
+        if core in off:
+            total[1] += len(e_off)
+        if core in served:
+            total[0] += len(bits(topo.mask(hand, core)))
+    for relay, m, on, off in switch:
+        e_on, e_off = split_engines(relay, on[0], off[0], topo)
+        if core == relay:
+            own[m].append((s.inp, N_PLANE))
+        total[m] += (len(e_on) if core in on else 0) + (len(e_off) if core in off else 0)
+    return own[0] + [(s.arr0, total[0])], own[1] + [(s.arr1, total[1])]
+
+
+def finish(g, core, T, topo, cable, switch, root):
     s = T.sem
     if core == root:
         make_h(g, T)
@@ -188,18 +243,10 @@ def finish(g, core, T, topo, routes, root):
     g.vector.wait_ge(s.lw2, 16)
     g.vector.quantize_mx(T.w2q[:], T.w2p[:], T.w2s[:]).then_inc(s.qw2, 1)
     g.tensor.wait_ge(s.qw2, 1)
-    if core == root:
-        g.tensor.wait_ge(s.qh0, 1)
-        g.tensor.wait_ge(s.qh1, 1)
-    else:
-        total = 0
-        for relay, u, on, off in routes:
-            e_on, e_off = split_engines(relay, on[0], off[0], topo)
-            if core == relay:
-                g.tensor.wait_ge(s.inp, arrival(u))
-            total += (len(e_on) if core in on else 0) + (len(e_off) if core in off else 0)
-        g.tensor.wait_ge(s.arr, total)
-    for m, sem in ((0, s.y0), (1, s.y1)):
+    waits = ([(s.qh0, 1)], [(s.qh1, 1)]) if core == root else landing(core, T, topo, cable, switch)
+    for m, sem in ((1, s.y1), (0, s.y0)):
+        for w, n in waits[m]:
+            g.tensor.wait_ge(w, n)
         c = slice(NC * m, NC * m + NC)
         g.tensor.matmul_mx(T.yp[:, 512 * m:512 * m + NC], T.w2q[:], T.w2p[:], T.hq[:, c], T.hp[:, c], True, True).then_inc(sem, 1)
     g.vector.wait_ge(s.y0, 1)

@@ -3,10 +3,12 @@ from concourse.mybir import dt, AluOpType, ActivationFunctionType
 
 C = 0.029
 NC = 128
-CABLE = 4
-WORDS = NC // CABLE
 WORLD = 512
 CODES, PLANE = "float8_e4m3fn_x4", "uint8"
+QUARTERS = 4
+WORDS = NC // QUARTERS
+P = QUARTERS
+RELAYED, DIRECT = (0, 1, 2), (3, P)
 
 SCRATCH = {
     "xs": ("sbuf", [128, 1024], "bfloat16"),
@@ -25,17 +27,17 @@ SCRATCH = {
     "z": ("psum", [128, 2048], "float32"),
     "yp": ("psum", [128, 1024], "float32"),
 }
-SEMAPHORES = ["lx", "lw1", "lw2", "qx0", "qx1", "qw10", "qw11", "qw2", "z00", "z01", "z10", "z11", "s0", "s1", "v0", "v1", "qh0", "qh1",
-              "early", "inp", "arr0", "arr1", "sent", "y0", "y1", "c0", "c1", "st0", "st1"]
+SEMAPHORES = ["lx0", "lx1", "lw10", "lw11", "lw2", "qx0", "qx1", "qw10", "qw11", "qw2", "z00", "z01", "z10", "z11",
+              "s0", "s1", "v0", "v1", "qh0", "qh1", "arr0", "arr1", "sent", "y0", "y1", "c0", "c1", "st0", "st1"]
+SEMAPHORES += ["pass%d%d" % (m, u) for m in (0, 1) for u in range(QUARTERS + 1)]
 
 
-def codes(T, m, u):
+def view(T, piece):
+    m, u = piece
+    if u == P:
+        return T.hp[:, NC * m:NC * m + NC]
     a = NC * m + WORDS * u
     return T.hq[:, a:a + WORDS].bitcast(dt.uint8)
-
-
-def plane(T, m):
-    return T.hp[:, NC * m:NC * m + NC]
 
 
 def bits(mask):
@@ -69,122 +71,146 @@ def plan(T, topo):
     diagonal = at(lambda c: not same_rack(c, root) and not topo.may_write(root, c))
     used = {root}
 
-    def take(groups, keys):
-        free = [c for key in keys for c in groups[key] if c not in used]
-        relay = sorted(free, key=lambda c: T.rank_of(c) is None)[0]
-        used.add(relay)
-        return relay
+    def take(ranks, keys):
+        groups = pairs_of(ranks[0], topo)
+        free = [c for key in sorted(keys(groups)) for c in groups[key] if c not in used]
+        core = sorted(free, key=lambda c: T.rank_of(c) is None)[0]
+        used.add(core)
+        return core
+
+    def cable_of(ranks, u):
+        groups = pairs_of(ranks[0], topo)
+        return [key for key in sorted(groups) if root not in groups[key]][u]
+    on_die = {u: (lambda groups, d=d: [key for key in groups if key[0] == d]) for d, u in enumerate(reversed(DIRECT))}
+    near = {u: take(home, lambda groups: [cable_of(home, u)]) for u in RELAYED}
+    away = {u: take(side, lambda groups: [cable_of(side, u)]) for u in RELAYED}
+    near.update({u: take(home, on_die[u]) for u in DIRECT})
+    away.update({u: take(across, on_die[u]) for u in DIRECT})
+    across_hand = {u: take(across, lambda groups: groups) for u in RELAYED}
+    diagonal_hand = {u: take(diagonal, lambda groups: groups) for u in RELAYED}
+    diagonal_hand.update({u: diagonal_hand[RELAYED[k]] for k, u in enumerate(DIRECT)})
+
+    far = topo.mask(root, side[0])
+    e_in, e_out = bits(topo.mask(root, home[0]) & ~far), bits(far)
+    calls = {}
+
+    def call(core, waits, *transfers):
+        calls.setdefault(core, []).append((waits, list(transfers)))
 
     def others(ranks, c):
         return [d for d in ranks if d != c]
-    firsts = []
-    for ranks, far in ((home, across), (side, diagonal)):
-        groups = pairs_of(ranks[0], topo)
-        firsts += [(take(groups, [key]), u, ranks, far) for u, key in enumerate(sorted(groups))]
-    switch = []
-    for ranks, far in ((home, side), (across, diagonal)):
-        groups = pairs_of(ranks[0], topo)
-        for m in (0, 1):
-            relay = take(groups, [key for key in sorted(groups) if key[0] == m])
-            switch.append((relay, m, others(ranks, relay), far))
-    cable = []
-    for relay, u, ranks, far in firsts:
-        groups = pairs_of(far[0], topo)
-        hand = take(groups, sorted(groups))
-        cable.append((relay, u, others(ranks, relay), far, hand, others(far, hand)))
-    return cable, switch
+
+    def deal(m, pieces, to, engines, first, n):
+        return [([to[u]], (m, u), engines[first + n * k:first + n * k + n]) for k, u in enumerate(pieces)]
+    call(root, (0, None), *(deal(0, RELAYED, away, e_out, 0, 2) + deal(0, DIRECT, away, e_out, 6, 1)))
+    call(root, (0, None), *(deal(0, RELAYED, near, e_in, 0, 2) + deal(0, DIRECT, near, e_in, 6, 1)))
+    call(root, (1, None), *(deal(1, RELAYED, away, e_out, 0, 2) + deal(1, RELAYED, near, e_in, 0, 2)))
+    call(root, (1, None), *(deal(1, DIRECT, away, e_out, 0, 4) + deal(1, DIRECT, near, e_in, 0, 4)))
+    for m in (0, 1):
+        e_hand = e_in if m == 0 else e_in + e_out
+        for u in RELAYED:
+            p = (m, u)
+            for relay, ranks, over, hand in ((near[u], home, across, across_hand[u]), (away[u], side, diagonal, diagonal_hand[u])):
+                call(relay, p, ([hand], p, e_out[0:4]))
+                call(relay, p, (others(ranks, relay), p, e_in))
+                call(hand, p, (others(over, hand), p, e_hand))
+        for u in DIRECT:
+            p = (m, u)
+            for relay, ranks, over in ((near[u], home, side), (away[u], across, diagonal)):
+                inside, outside = (others(ranks, relay), p, e_in), (over, p, e_out)
+                if m == 0:
+                    call(relay, p, outside)
+                    call(relay, p, inside)
+                elif over is side:
+                    call(relay, p, outside, inside)
+                else:
+                    hand = diagonal_hand[u]
+                    call(relay, p, ([hand], p, e_out), inside)
+                    call(hand, p, (others(over, hand), p, e_hand))
+    return calls
 
 
-def dst(topo, d, src):
-    rid, pid = topo.addr(d, src)
-    return DstId(rid=rid, pnc=pid)
-
-
-def split_engines(src, on, off, topo):
-    away = topo.mask(src, off)
-    return bits(topo.mask(src, on) & ~away), bits(away)
-
-
-def transfer(topo, src, dests, view, engines, sem):
-    return RemoteDMATransfer(dst_ids=[dst(topo, d, src) for d in dests], dma_engine_mask=mask_of(engines), remote_sem=sem,
-                             srcs=[view], dsts=[view for d in dests])
-
-
-N_CODES, N_PLANE = 2, 4
+PLANS = {}
 
 
 def rank_program(g, core, T, topo):
     root = T.cores[T.root]
-    cable, switch = plan(T, topo)
-    s = T.sem
+    if root not in PLANS:
+        PLANS[root] = plan(T, topo)
+    calls, s = PLANS[root], T.sem
+
+    def lands_on(d, piece):
+        passed = any(waits == piece for waits, _ in calls.get(d, ()))
+        return "pass%d%d" % piece if passed else "arr%d" % piece[0]
+    landing = {}
+    for sends in calls.values():
+        for _, transfers in sends:
+            for ds, piece, engines in transfers:
+                if core in ds:
+                    name = lands_on(core, piece)
+                    landing[name] = (piece[0], landing.get(name, (0, 0))[1] + len(engines))
     if T.rank_of(core) is not None:
-        finish(g, core, T, topo, cable, switch, root)
-    if core == root:
-        root_send(g, core, T, topo, cable, switch)
-    for relay, u, on, off, hand, served in cable:
-        if core == relay:
-            e_on, e_off = split_engines(core, on[0], off[0], topo)
-            g.wait_ge(s.early, N_CODES)
-            g.remote_dma_fused([transfer(topo, core, [hand], codes(T, 0, u), e_off, s.early)], local_sem=s.sent)
-            g.wait_ge(s.inp, N_CODES)
-            g.remote_dma_fused([transfer(topo, core, off, codes(T, 1, u), e_off, s.arr1),
-                                transfer(topo, core, on, codes(T, 1, u), e_on, s.arr1)], local_sem=s.sent)
-            g.remote_dma_fused([transfer(topo, core, on, codes(T, 0, u), e_on, s.arr0)], local_sem=s.sent)
-            g.wait_ge(s.sent, 2 * (len(e_on) + len(e_off)))
-        if core == hand:
-            engines = bits(topo.mask(core, served[0]))
-            g.wait_ge(s.early, len(split_engines(relay, on[0], off[0], topo)[1]))
-            g.remote_dma_fused([transfer(topo, core, served, codes(T, 0, u), engines, s.arr0)], local_sem=s.sent)
-            g.wait_ge(s.sent, len(engines))
-    for relay, m, on, off in switch:
-        if core == relay:
-            e_on, e_off = split_engines(core, on[0], off[0], topo)
-            sem = (s.arr0, s.arr1)[m]
-            g.wait_ge(s.inp, N_PLANE)
-            g.remote_dma_fused([transfer(topo, core, off, plane(T, m), e_off, sem),
-                                transfer(topo, core, on, plane(T, m), e_on, sem)], local_sem=s.sent)
-            g.wait_ge(s.sent, len(e_on) + len(e_off))
-
-
-def root_send(g, core, T, topo, cable, switch):
-    s = T.sem
-
-    def by_host(routes):
-        near = [r for r in routes if topo.host(r[0]) == topo.host(core)]
-        return (sorted(near, key=lambda r: topo.die(r[0]) == topo.die(core)),
-                [r for r in routes if topo.host(r[0]) != topo.host(core)])
-    e_on, e_off = split_engines(core, cable[0][0], by_host(cable)[1][0][0], topo)
-    turns = e_on[0::2] + e_on[1::2]
-    for ready, routes, n, view, sem in ((s.qh0, cable, N_CODES, lambda k: codes(T, 0, k), s.early),
-                                        (s.qh1, cable, N_CODES, lambda k: codes(T, 1, k), s.inp),
-                                        (None, switch, N_PLANE, lambda k: plane(T, k), s.inp)):
-        if ready is not None:
-            g.wait_ge(ready, 1)
-        near, away = by_host(routes)
-        g.remote_dma_fused([transfer(topo, core, [r[0]], view(r[1]), engines[n * k:n * k + n], sem)
-                            for part, engines in ((away, e_off), (near, turns)) for k, r in enumerate(part)], local_sem=s.sent)
-    g.wait_ge(s.sent, 3 * (len(e_on) + len(e_off)))
+        if core == root:
+            make_h(g, T)
+            waits = ([(s.qh0, 1)], [(s.qh1, 1)])
+        else:
+            waits = [[(s[name], n) for name, (m, n) in sorted(landing.items()) if m == tile] for tile in (0, 1)]
+        finish(g, T, waits)
+    sent, ready = 0, set()
+    for piece, transfers in calls.get(core, ()):
+        if piece not in ready:
+            ready.add(piece)
+            if core == root:
+                g.wait_ge((s.qh0, s.qh1)[piece[0]], 1)
+            else:
+                name = lands_on(core, piece)
+                g.wait_ge(s[name], landing[name][1])
+        out = []
+        for ds, p, engines in transfers:
+            ids = [DstId(rid=rid, pnc=pid) for rid, pid in (topo.addr(d, core) for d in ds)]
+            out.append(RemoteDMATransfer(dst_ids=ids, dma_engine_mask=mask_of(engines), remote_sem=s[lands_on(ds[0], p)],
+                                         srcs=[view(T, p)], dsts=[view(T, p) for d in ds]))
+            sent += len(engines)
+        g.remote_dma_fused(out, local_sem=s.sent)
+    if sent:
+        g.wait_ge(s.sent, sent)
 
 
 def make_h(g, T):
     s = T.sem
-    g.sync.dma_start(T.xs[:], T.x[:]).then_inc(s.lx, 16)
-    g.scalar.dma_start(T.w1s[:], T.w1[:]).then_inc(s.lw1, 16)
+    lo, hi = slice(0, 512), slice(512, 1024)
+    g.sync.dma_start(T.xs[:, lo], T.x[:, lo]).then_inc(s.lx0, 16)
+    g.scalar.dma_start(T.w1s[:, lo], T.w1[:, lo]).then_inc(s.lw10, 16)
+    g.sync.dma_start(T.w1s[:, hi], T.w1[:, hi]).then_inc(s.lw11, 16)
+    g.sync.dma_start(T.xs[:, hi], T.x[:, hi]).then_inc(s.lx1, 16)
 
     def quantise(q, p, i, src, sem):
         g.vector.quantize_mx(q[:, NC * i:NC * i + NC], p[:, NC * i:NC * i + NC],
                              src[:, 4 * NC * i:4 * NC * i + 4 * NC]).then_inc(sem, 1)
-    g.vector.wait_ge(s.lx, 16)
-    quantise(T.xq, T.xp, 0, T.xs, s.qx0)
-    g.vector.wait_ge(s.lw1, 16)
-    quantise(T.w1q, T.w1p, 0, T.w1s, s.qw10)
-    quantise(T.w1q, T.w1p, 1, T.w1s, s.qw11)
-    quantise(T.xq, T.xp, 1, T.xs, s.qx1)
 
     def product(i, m, sem):
         b = 512 * (2 * i + m)
         w, c = slice(NC * i, NC * i + NC), slice(NC * m, NC * m + NC)
         g.tensor.matmul_mx(T.z[:, b:b + NC], T.w1q[:, w], T.w1p[:, w], T.xq[:, c], T.xp[:, c], True, True).then_inc(sem, 1)
+
+    def signs(m, zs, zv, ss, sv, qh):
+        lo, hi = 512 * m, 512 * m + 512
+        z0, z1 = T.z[:, lo:lo + NC], T.z[:, 1024 + lo:1024 + lo + NC]
+        g.scalar.wait_ge(zs, 1)
+        g.scalar.activation(T.h[:, lo:hi:4], z0, ActivationFunctionType.Relu, scale=C).then_inc(ss, 1)
+        g.scalar.activation(T.h[:, lo + 1:hi:4], z0, ActivationFunctionType.Relu, scale=-C).then_inc(ss, 1)
+        g.vector.wait_ge(zv, 1)
+        g.vector.tensor_scalar(T.h[:, lo + 2:hi:4], z1, 0.0, C, AluOpType.max, AluOpType.mult).then_inc(sv, 1)
+        g.vector.tensor_scalar(T.h[:, lo + 3:hi:4], z1, -C, 0.0, AluOpType.mult, AluOpType.max).then_inc(sv, 1)
+        g.vector.wait_ge(sv, 2)
+        g.vector.wait_ge(ss, 2)
+        quantise(T.hq, T.hp, m, T.h, qh)
+    g.vector.wait_ge(s.lx0, 16)
+    quantise(T.xq, T.xp, 0, T.xs, s.qx0)
+    g.vector.wait_ge(s.lw10, 16)
+    quantise(T.w1q, T.w1p, 0, T.w1s, s.qw10)
+    g.vector.wait_ge(s.lw11, 16)
+    quantise(T.w1q, T.w1p, 1, T.w1s, s.qw11)
     g.tensor.wait_ge(s.qx0, 1)
     g.tensor.wait_ge(s.qw10, 1)
     product(0, 0, s.z00)
@@ -193,69 +219,32 @@ def make_h(g, T):
     g.tensor.wait_ge(s.qx1, 1)
     product(0, 1, s.z01)
     product(1, 1, s.z11)
-
-    for m, zv, zs, ss, sv, qh in ((0, s.z00, s.z10, s.s0, s.v0, s.qh0), (1, s.z01, s.z11, s.s1, s.v1, s.qh1)):
-        lo, hi = 512 * m, 512 * m + 512
-        z0, z1 = T.z[:, lo:lo + NC], T.z[:, 1024 + lo:1024 + lo + NC]
-        g.vector.wait_ge(zv, 1)
-        g.vector.tensor_scalar(T.h[:, lo:hi:4], z0, 0.0, C, AluOpType.max, AluOpType.mult).then_inc(sv, 1)
-        g.vector.tensor_scalar(T.h[:, lo + 1:hi:4], z0, -C, 0.0, AluOpType.mult, AluOpType.max).then_inc(sv, 1)
-        g.scalar.wait_ge(zs, 1)
-        g.scalar.activation(T.h[:, lo + 2:hi:4], z1, ActivationFunctionType.Relu, scale=C).then_inc(ss, 1)
-        g.scalar.activation(T.h[:, lo + 3:hi:4], z1, ActivationFunctionType.Relu, scale=-C).then_inc(ss, 1)
-        g.vector.wait_ge(sv, 2)
-        g.vector.wait_ge(ss, 2)
-        quantise(T.hq, T.hp, m, T.h, qh)
+    signs(0, s.z00, s.z10, s.s0, s.v0, s.qh0)
+    g.vector.wait_ge(s.lx1, 16)
+    quantise(T.xq, T.xp, 1, T.xs, s.qx1)
+    signs(1, s.z01, s.z11, s.s1, s.v1, s.qh1)
+    for sem in (s.lx0, s.lw10, s.lw11, s.lx1):
+        g.sync.wait_ge(sem, 16)
 
 
-def landing(core, T, topo, cable, switch):
+def finish(g, T, waits):
     s = T.sem
-    own, total = ([], []), [0, 0]
-    for relay, u, on, off, hand, served in cable:
-        e_on, e_off = split_engines(relay, on[0], off[0], topo)
-        if core == relay:
-            own[0].append((s.early, N_CODES))
-            own[1].append((s.inp, N_CODES))
-        if core == hand:
-            own[0].append((s.early, len(e_off)))
-        if core in on:
-            total[0] += len(e_on)
-            total[1] += len(e_on)
-        if core in off:
-            total[1] += len(e_off)
-        if core in served:
-            total[0] += len(bits(topo.mask(hand, core)))
-    for relay, m, on, off in switch:
-        e_on, e_off = split_engines(relay, on[0], off[0], topo)
-        if core == relay:
-            own[m].append((s.inp, N_PLANE))
-        total[m] += (len(e_on) if core in on else 0) + (len(e_off) if core in off else 0)
-    return own[0] + [(s.arr0, total[0])], own[1] + [(s.arr1, total[1])]
-
-
-def finish(g, core, T, topo, cable, switch, root):
-    s = T.sem
-    if core == root:
-        make_h(g, T)
-        g.sync.wait_ge(s.lx, 16)
-        g.sync.wait_ge(s.lw1, 16)
     g.sync.dma_start(T.w2s[:], T.w2[:]).then_inc(s.lw2, 16)
     g.vector.wait_ge(s.lw2, 16)
     g.vector.quantize_mx(T.w2q[:], T.w2p[:], T.w2s[:]).then_inc(s.qw2, 1)
     g.tensor.wait_ge(s.qw2, 1)
-    waits = ([(s.qh0, 1)], [(s.qh1, 1)]) if core == root else landing(core, T, topo, cable, switch)
-    for m, sem in ((1, s.y1), (0, s.y0)):
+    for m, sem in ((0, s.y0), (1, s.y1)):
         for w, n in waits[m]:
             g.tensor.wait_ge(w, n)
         c = slice(NC * m, NC * m + NC)
         g.tensor.matmul_mx(T.yp[:, 512 * m:512 * m + NC], T.w2q[:], T.w2p[:], T.hq[:, c], T.hp[:, c], True, True).then_inc(sem, 1)
-    g.vector.wait_ge(s.y0, 1)
-    g.vector.tensor_copy(T.ys[:, 0:NC], T.yp[:, 0:NC]).then_inc(s.c0, 1)
-    g.sync.wait_ge(s.c0, 1)
-    g.sync.dma_start(T.y[:, 0:NC], T.ys[:, 0:NC]).then_inc(s.st0, 16)
-    g.sync.wait_ge(s.st0, 16)
-    g.scalar.wait_ge(s.y1, 1)
-    g.scalar.activation(T.ys[:, NC:2 * NC], T.yp[:, 512:512 + NC], ActivationFunctionType.Copy).then_inc(s.c1, 1)
-    g.scalar.wait_ge(s.c1, 1)
-    g.scalar.dma_start(T.y[:, NC:2 * NC], T.ys[:, NC:2 * NC]).then_inc(s.st1, 16)
-    g.scalar.wait_ge(s.st1, 16)
+    g.scalar.wait_ge(s.y0, 1)
+    g.scalar.activation(T.ys[:, 0:NC], T.yp[:, 0:NC], ActivationFunctionType.Copy).then_inc(s.c0, 1)
+    g.scalar.wait_ge(s.c0, 1)
+    g.scalar.dma_start(T.y[:, 0:NC], T.ys[:, 0:NC]).then_inc(s.st0, 16)
+    g.scalar.wait_ge(s.st0, 16)
+    g.vector.wait_ge(s.y1, 1)
+    g.vector.tensor_copy(T.ys[:, NC:2 * NC], T.yp[:, 512:512 + NC]).then_inc(s.c1, 1)
+    g.sync.wait_ge(s.c1, 1)
+    g.sync.dma_start(T.y[:, NC:2 * NC], T.ys[:, NC:2 * NC]).then_inc(s.st1, 16)
+    g.sync.wait_ge(s.st1, 16)

from concourse.bass import DstId, RemoteDMATransfer
from concourse.mybir import dt, AluOpType, ActivationFunctionType

C = 0.029
NC = 128
WORLD = 512
CODES, PLANE = "float8_e4m3fn_x4", "uint8"
QUARTERS = 4
WORDS = NC // QUARTERS
P = QUARTERS
RELAYED, DIRECT = (0, 1, 2), (3, P)

SCRATCH = {
    "xs": ("sbuf", [128, 1024], "bfloat16"),
    "w1s": ("sbuf", [128, 1024], "bfloat16"),
    "w2s": ("sbuf", [128, 512], "bfloat16"),
    "h": ("sbuf", [128, 1024], "bfloat16"),
    "xq": ("sbuf", [128, 256], CODES),
    "xp": ("sbuf", [128, 256], PLANE),
    "w1q": ("sbuf", [128, 256], CODES),
    "w1p": ("sbuf", [128, 256], PLANE),
    "w2q": ("sbuf", [128, 128], CODES),
    "w2p": ("sbuf", [128, 128], PLANE),
    "hq": ("sbuf", [128, 256], CODES),
    "hp": ("sbuf", [128, 256], PLANE),
    "ys": ("sbuf", [128, 256], "float32"),
    "z": ("psum", [128, 2048], "float32"),
    "yp": ("psum", [128, 1024], "float32"),
}
SEMAPHORES = ["lx0", "lx1", "lw10", "lw11", "lw2", "qx0", "qx1", "qw10", "qw11", "qw2", "z00", "z01", "z10", "z11",
              "s0", "s1", "v0", "v1", "qh0", "qh1", "arr0", "arr1", "sent", "y0", "y1", "c0", "c1", "st0", "st1"]
SEMAPHORES += ["pass%d%d" % (m, u) for m in (0, 1) for u in range(QUARTERS + 1)]


def view(T, piece):
    m, u = piece
    if u == P:
        return T.hp[:, NC * m:NC * m + NC]
    a = NC * m + WORDS * u
    return T.hq[:, a:a + WORDS].bitcast(dt.uint8)


def bits(mask):
    return [b for b in range(16) if mask >> b & 1]


def mask_of(engines):
    return sum(1 << e for e in engines)


def pairs_of(c, topo):
    groups = {}
    for d in range(WORLD):
        if topo.host(d) == topo.host(c) and topo.chip(d) == topo.chip(c):
            owner = any(topo.mates(d, m) and topo.may_write(d, m) for m in range(WORLD))
            groups.setdefault((topo.die(d), owner), []).append(d)
    return groups


def plan(T, topo):
    root = T.cores[T.root]

    def at(test):
        return [c for c in T.cores if c != root and test(c)]

    def same_rack(a, b):
        return topo.rack(topo.host(a)) == topo.rack(topo.host(b))
    home = at(lambda c: topo.host(c) == topo.host(root))
    side = at(lambda c: topo.host(c) != topo.host(root) and same_rack(c, root))
    across = at(lambda c: not same_rack(c, root) and topo.may_write(root, c))
    diagonal = at(lambda c: not same_rack(c, root) and not topo.may_write(root, c))
    used = {root}

    def take(ranks, keys):
        groups = pairs_of(ranks[0], topo)
        free = [c for key in sorted(keys(groups)) for c in groups[key] if c not in used]
        core = sorted(free, key=lambda c: T.rank_of(c) is None)[0]
        used.add(core)
        return core

    def cable_of(ranks, u):
        groups = pairs_of(ranks[0], topo)
        return [key for key in sorted(groups) if root not in groups[key]][u]
    on_die = {u: (lambda groups, d=d: [key for key in groups if key[0] == d]) for d, u in enumerate(reversed(DIRECT))}
    near = {u: take(home, lambda groups: [cable_of(home, u)]) for u in RELAYED}
    away = {u: take(side, lambda groups: [cable_of(side, u)]) for u in RELAYED}
    near.update({u: take(home, on_die[u]) for u in DIRECT})
    away.update({u: take(across, on_die[u]) for u in DIRECT})
    across_hand = {u: take(across, lambda groups: groups) for u in RELAYED}
    diagonal_hand = {u: take(diagonal, lambda groups: groups) for u in RELAYED}
    diagonal_hand.update({u: diagonal_hand[RELAYED[k]] for k, u in enumerate(DIRECT)})

    far = topo.mask(root, side[0])
    e_in, e_out = bits(topo.mask(root, home[0]) & ~far), bits(far)
    calls = {}

    def call(core, waits, *transfers):
        calls.setdefault(core, []).append((waits, list(transfers)))

    def others(ranks, c):
        return [d for d in ranks if d != c]

    def deal(m, pieces, to, engines, first, n):
        return [([to[u]], (m, u), engines[first + n * k:first + n * k + n]) for k, u in enumerate(pieces)]
    call(root, (0, None), *(deal(0, RELAYED, away, e_out, 0, 2) + deal(0, DIRECT, away, e_out, 6, 1)))
    call(root, (0, None), *(deal(0, RELAYED, near, e_in, 0, 2) + deal(0, DIRECT, near, e_in, 6, 1)))
    call(root, (1, None), *(deal(1, RELAYED, away, e_out, 0, 2) + deal(1, RELAYED, near, e_in, 0, 2)))
    call(root, (1, None), *(deal(1, DIRECT, away, e_out, 0, 4) + deal(1, DIRECT, near, e_in, 0, 4)))
    for m in (0, 1):
        e_hand = e_in if m == 0 else e_in + e_out
        for u in RELAYED:
            p = (m, u)
            for relay, ranks, over, hand in ((near[u], home, across, across_hand[u]), (away[u], side, diagonal, diagonal_hand[u])):
                call(relay, p, ([hand], p, e_out[0:4]))
                call(relay, p, (others(ranks, relay), p, e_in))
                call(hand, p, (others(over, hand), p, e_hand))
        for u in DIRECT:
            p = (m, u)
            for relay, ranks, over in ((near[u], home, side), (away[u], across, diagonal)):
                inside, outside = (others(ranks, relay), p, e_in), (over, p, e_out)
                if m == 0:
                    call(relay, p, outside)
                    call(relay, p, inside)
                elif over is side:
                    call(relay, p, outside, inside)
                else:
                    hand = diagonal_hand[u]
                    call(relay, p, ([hand], p, e_out), inside)
                    call(hand, p, (others(over, hand), p, e_hand))
    return calls


PLANS = {}


def rank_program(g, core, T, topo):
    root = T.cores[T.root]
    if root not in PLANS:
        PLANS[root] = plan(T, topo)
    calls, s = PLANS[root], T.sem

    def lands_on(d, piece):
        passed = any(waits == piece for waits, _ in calls.get(d, ()))
        return "pass%d%d" % piece if passed else "arr%d" % piece[0]
    landing = {}
    for sends in calls.values():
        for _, transfers in sends:
            for ds, piece, engines in transfers:
                if core in ds:
                    name = lands_on(core, piece)
                    landing[name] = (piece[0], landing.get(name, (0, 0))[1] + len(engines))
    if T.rank_of(core) is not None:
        if core == root:
            make_h(g, T)
            waits = ([(s.qh0, 1)], [(s.qh1, 1)])
        else:
            waits = [[(s[name], n) for name, (m, n) in sorted(landing.items()) if m == tile] for tile in (0, 1)]
        finish(g, T, waits)
    sent, ready = 0, set()
    for piece, transfers in calls.get(core, ()):
        if piece not in ready:
            ready.add(piece)
            if core == root:
                g.wait_ge((s.qh0, s.qh1)[piece[0]], 1)
            else:
                name = lands_on(core, piece)
                g.wait_ge(s[name], landing[name][1])
        out = []
        for ds, p, engines in transfers:
            ids = [DstId(rid=rid, pnc=pid) for rid, pid in (topo.addr(d, core) for d in ds)]
            out.append(RemoteDMATransfer(dst_ids=ids, dma_engine_mask=mask_of(engines), remote_sem=s[lands_on(ds[0], p)],
                                         srcs=[view(T, p)], dsts=[view(T, p) for d in ds]))
            sent += len(engines)
        g.remote_dma_fused(out, local_sem=s.sent)
    if sent:
        g.wait_ge(s.sent, sent)


def make_h(g, T):
    s = T.sem
    lo, hi = slice(0, 512), slice(512, 1024)
    g.sync.dma_start(T.xs[:, lo], T.x[:, lo]).then_inc(s.lx0, 16)
    g.scalar.dma_start(T.w1s[:, lo], T.w1[:, lo]).then_inc(s.lw10, 16)
    g.sync.dma_start(T.w1s[:, hi], T.w1[:, hi]).then_inc(s.lw11, 16)
    g.sync.dma_start(T.xs[:, hi], T.x[:, hi]).then_inc(s.lx1, 16)

    def quantise(q, p, i, src, sem):
        g.vector.quantize_mx(q[:, NC * i:NC * i + NC], p[:, NC * i:NC * i + NC],
                             src[:, 4 * NC * i:4 * NC * i + 4 * NC]).then_inc(sem, 1)

    def product(i, m, sem):
        b = 512 * (2 * i + m)
        w, c = slice(NC * i, NC * i + NC), slice(NC * m, NC * m + NC)
        g.tensor.matmul_mx(T.z[:, b:b + NC], T.w1q[:, w], T.w1p[:, w], T.xq[:, c], T.xp[:, c], True, True).then_inc(sem, 1)

    def signs(m, zs, zv, ss, sv, qh):
        lo, hi = 512 * m, 512 * m + 512
        z0, z1 = T.z[:, lo:lo + NC], T.z[:, 1024 + lo:1024 + lo + NC]
        g.scalar.wait_ge(zs, 1)
        g.scalar.activation(T.h[:, lo:hi:4], z0, ActivationFunctionType.Relu, scale=C).then_inc(ss, 1)
        g.scalar.activation(T.h[:, lo + 1:hi:4], z0, ActivationFunctionType.Relu, scale=-C).then_inc(ss, 1)
        g.vector.wait_ge(zv, 1)
        g.vector.tensor_scalar(T.h[:, lo + 2:hi:4], z1, 0.0, C, AluOpType.max, AluOpType.mult).then_inc(sv, 1)
        g.vector.tensor_scalar(T.h[:, lo + 3:hi:4], z1, -C, 0.0, AluOpType.mult, AluOpType.max).then_inc(sv, 1)
        g.vector.wait_ge(sv, 2)
        g.vector.wait_ge(ss, 2)
        quantise(T.hq, T.hp, m, T.h, qh)
    g.vector.wait_ge(s.lx0, 16)
    quantise(T.xq, T.xp, 0, T.xs, s.qx0)
    g.vector.wait_ge(s.lw10, 16)
    quantise(T.w1q, T.w1p, 0, T.w1s, s.qw10)
    g.vector.wait_ge(s.lw11, 16)
    quantise(T.w1q, T.w1p, 1, T.w1s, s.qw11)
    g.tensor.wait_ge(s.qx0, 1)
    g.tensor.wait_ge(s.qw10, 1)
    product(0, 0, s.z00)
    g.tensor.wait_ge(s.qw11, 1)
    product(1, 0, s.z10)
    g.tensor.wait_ge(s.qx1, 1)
    product(0, 1, s.z01)
    product(1, 1, s.z11)
    signs(0, s.z00, s.z10, s.s0, s.v0, s.qh0)
    g.vector.wait_ge(s.lx1, 16)
    quantise(T.xq, T.xp, 1, T.xs, s.qx1)
    signs(1, s.z01, s.z11, s.s1, s.v1, s.qh1)
    for sem in (s.lx0, s.lw10, s.lw11, s.lx1):
        g.sync.wait_ge(sem, 16)


def finish(g, T, waits):
    s = T.sem
    g.sync.dma_start(T.w2s[:], T.w2[:]).then_inc(s.lw2, 16)
    g.vector.wait_ge(s.lw2, 16)
    g.vector.quantize_mx(T.w2q[:], T.w2p[:], T.w2s[:]).then_inc(s.qw2, 1)
    g.tensor.wait_ge(s.qw2, 1)
    for m, sem in ((0, s.y0), (1, s.y1)):
        for w, n in waits[m]:
            g.tensor.wait_ge(w, n)
        c = slice(NC * m, NC * m + NC)
        g.tensor.matmul_mx(T.yp[:, 512 * m:512 * m + NC], T.w2q[:], T.w2p[:], T.hq[:, c], T.hp[:, c], True, True).then_inc(sem, 1)
    g.scalar.wait_ge(s.y0, 1)
    g.scalar.activation(T.ys[:, 0:NC], T.yp[:, 0:NC], ActivationFunctionType.Copy).then_inc(s.c0, 1)
    g.scalar.wait_ge(s.c0, 1)
    g.scalar.dma_start(T.y[:, 0:NC], T.ys[:, 0:NC]).then_inc(s.st0, 16)
    g.scalar.wait_ge(s.st0, 16)
    g.vector.wait_ge(s.y1, 1)
    g.vector.tensor_copy(T.ys[:, NC:2 * NC], T.yp[:, 512:512 + NC]).then_inc(s.c1, 1)
    g.sync.wait_ge(s.c1, 1)
    g.sync.dma_start(T.y[:, NC:2 * NC], T.ys[:, NC:2 * NC]).then_inc(s.st1, 16)
    g.sync.wait_ge(s.st1, 16)
